import numpy as np, ml_dtypes
CORES = [2,3,42,43,82,83,122,123]
N = 8
BF = ml_dtypes.bfloat16
def gentries(a):
    return np.ascontiguousarray(a.reshape(8, 16, -1).transpose(0, 2, 1)).reshape(8, -1)
def gtable(e):
    e = np.asarray(e); return np.ascontiguousarray(e.reshape(8, -1, 16).transpose(0, 2, 1)).reshape(128, -1).astype(np.int32)
H, E, L = 4096, 64, 2
M = (N - 1) * E
def slot(r, q):
    return q - (1 if q > r else 0)
def flat(a):
    return np.ascontiguousarray(np.asarray(a).astype(np.int64).transpose(1, 0, 2)).reshape(8, -1)
def perms(rng):
    return np.argsort(rng.random((N, 8, H)), axis=-1)
def mesh(c, w, lens):
    nx, pv, tw = np.empty((N, 8, H), np.int64), np.empty((N, 8, H), np.int64), np.empty((N, 8, H), np.int64)
    for r in range(N):
        for g in range(8):
            e = np.add.accumulate(lens[r, g]); e = np.append(e[e < H], H); s = np.append(0, e[:-1])
            k = np.arange(1, H + 1); k[e - 1] = s; a = w[r, g]
            nx[r, g, a] = H * r + a[k]; pv[r, g, a[k]] = H * r + a
            b = c[r, g, M:].reshape(-1, 2); tw[r, g, b] = H * r + b[:, ::-1]
            for q in range(N):
                if q != r:
                    i, j = E * slot(r, q), E * slot(q, r)
                    tw[r, g, c[r, g, i:i + E]] = H * q + c[q, g, j:j + E]
    return {"nxt": nx.astype(np.int32), "prv": pv.astype(np.int32), "twn": tw.astype(np.int32), "far": np.stack([gtable(c[r, :, :M]) for r in range(N)])}
def draw(v, c, w, lens):
    d = {"x": v.astype(np.float32).astype(BF)}; d.update(mesh(c, w, lens)); return d
def setup_inputs(rng):
    v = rng.integers(-31, 32, (N, 128, H))
    return draw(v, perms(rng), perms(rng), rng.integers(3, 9, (N, 8, H)))
def setup_inputs_long(rng):
    v = rng.integers(-31, 32, (N, 128, H)); k = (np.arange(N)[:, None] + np.arange(8) + rng.integers(0, 3)) % 3
    lens = rng.integers(1, 3, (N, 8, H)); lens[k == 0] = H
    lens = np.where((k == 2)[:, :, None], rng.integers(1, 201, (N, 8, H)), lens)
    return draw(v, perms(rng), perms(rng), lens)
def setup_inputs_near(rng):
    v = np.where(rng.random((N, 128, H)) < 0.875, 31, -31); a = np.arange(H)
    e = np.append(a[:M // 2], a[H - M // 2:]); mid = a[M // 2:H - M // 2]; c = np.empty((N, 8, H), np.int64); c[:, :, M:] = mid
    for r in range(N):
        for g in range(8): c[r, g, :M] = rng.permutation(e)
    w = np.broadcast_to(a, (N, 8, H))
    return draw(v, c, w, rng.integers(2, 6, (N, 8, H)))
def setup_inputs_hops(rng):
    v = rng.integers(-31, 32, (N, 128, H)); c = perms(rng); w = c.copy()
    for r in range(N):
        for g in range(4): w[r, g, :M] = rng.permutation(c[r, g, :M])
    return draw(v, c, w, rng.integers(3, 17, (N, 8, H)))
def setup_inputs_spread(rng):
    v = (rng.integers(-31, 32, (N, 128, H)) >> rng.integers(0, 5, (N, 1, H))) * (rng.random((N, 1, H)) > 0.0625)
    return draw(v, perms(rng), perms(rng), 2 ** rng.integers(0, 8, (N, 8, H)))
def check_inputs(d):
    bad = []
    try:
        v = np.asarray(d["x"]).astype(np.float32)
        if not (v.shape == (N, 128, H) and np.isfinite(v).all() and (np.abs(v) <= 31).all() and (v == np.floor(v)).all()): bad.append("x: whole numbers from -31 to 31")
        nx, pv, tw = [np.asarray(d[k]).astype(np.int64) for k in ("nxt", "prv", "twn")]
        own = np.broadcast_to(np.arange(N)[:, None, None], (N, 8, H))
        if not all(a.shape == (N, 8, H) and (a >= 0).all() and (a < N * H).all() for a in (nx, pv, tw)): return bad + ["nxt, prv, twn: range"]
        if not ((nx // H == own).all() and (pv // H == own).all()): bad.append("nxt, prv: same rank")
        n, p, t = flat(nx), flat(pv), flat(tw); me = np.arange(N * H)
        if any((p[g][n[g]] != me).any() or (n[g][p[g]] != me).any() for g in range(8)): bad.append("nxt and prv: one undoes the other")
        if any((t[g][t[g]] != me).any() or (t[g] == me).any() for g in range(8)): bad.append("twn: pairs")
        for r in range(N):
            for q in range(N):
                if q != r and (np.sum(tw[r] // H == q, axis=1) != E).any(): bad.append("twn: E far twins a pair")
        f = np.stack([gentries(np.asarray(a).astype(np.int64)) for a in d["far"]])
        if not (f.shape == (N, 8, M) and (f >= 0).all() and (f < H).all()): return bad + ["far: range"]
        u = np.sort(f, axis=-1)
        if (u[..., 1:] == u[..., :-1]).any(): bad.append("far: all different")
        for r in range(N):
            for q in range(N):
                if q != r:
                    i, j = E * slot(r, q), E * slot(q, r)
                    if any((tw[r, g][f[r, g, i:i + E]] != H * q + f[q, g, j:j + E]).any() for g in range(8)): bad.append("far: order")
    except Exception:
        bad.append("shapes")
    return bad
def reference(x, nxt, prv, twn, far):
    v = x.astype(np.float32).reshape(N, 8, 16, H).transpose(1, 2, 0, 3).reshape(8, 16, N * H)
    n, p, t = flat(nxt), flat(prv), flat(twn)
    for k in range(L):
        W = v.shape[2]; v2 = np.empty((8, 16, 2 * W), np.float32); n2, p2 = np.empty((8, 2 * W), np.int64), np.empty((8, 2 * W), np.int64)
        for g in range(8):
            m = v[g] + v[g][:, n[g]]
            v2[g, :, 0::2] = m; v2[g, :, 1::2] = m[:, n[g]]
            n2[g, 0::2] = 2 * n[g]; n2[g, 1::2] = 2 * p[g][t[g]] + 1
            p2[g, 0::2] = 2 * p[g]; p2[g, 1::2] = 2 * t[g][n[g]] + 1
        v, n, p = v2, n2, p2; t = np.broadcast_to(np.arange(2 * W) ^ 1, (8, 2 * W))
    y = v.reshape(8, 16, N, -1)[..., 1::2].transpose(2, 0, 1, 3)
    return {"y": np.ascontiguousarray(y).reshape(N, 128, -1).astype(BF), "nx": np.ascontiguousarray(n.reshape(8, N, -1).transpose(1, 0, 2)).astype(np.float32)}

@@ -1,0 +1,280 @@
+from concourse.bass import DstId, RemoteDMATransfer
+from concourse.mybir import dt, AluOpType, ActivationFunctionType
+
+H, E, NS = 4096, 64, 7
+M = NS * E
+HX = H + M
+BFD, F32, I32, U16 = "bfloat16", "float32", "int32", "uint16"
+SCRATCH = {"NX": ("sbuf", [128, 1024], F32), "EQ": ("sbuf", [128, 16, 16], BFD), "BM": ("sbuf", [128, 16], F32),
+           "Y": ("sbuf", [128, 2 * H], BFD), "FA": ("sbuf", [128, 28], I32), "SI": ("sbuf", [128, 64], F32)}
+for _k in ("X", "X2", "M2", "U2", "N3", "NN", "NT", "Q"):
+    SCRATCH[_k] = ("sbuf", [128, H], BFD)
+for _k in ("NW", "MX", "UX"):
+    SCRATCH[_k] = ("sbuf", [128, HX], BFD)
+for _k in ("NA", "PA", "TA"):
+    SCRATCH[_k] = ("sbuf", [128, 256], I32)
+for _k in ("NH", "NL", "PH", "PL", "TH", "TL", "TNH", "TNL", "PTH", "PTL"):
+    SCRATCH[_k] = ("sbuf", [128, 256], BFD)
+for _k in ("TMP", "TMP2"):
+    SCRATCH[_k] = ("sbuf", [128, 256], F32)
+for _k in ("D0", "D1"):
+    SCRATCH[_k] = ("sbuf", [128, 16, 128], BFD)
+for _k in ("LI", "LA"):
+    SCRATCH[_k] = ("sbuf", [128, 8], I32)
+for _k in ("LM", "HI", "OF", "BB"):
+    SCRATCH[_k] = ("sbuf", [128, 8], F32)
+for _k in ("C3", "R1", "RN", "XF", "MF", "EE", "VV"):
+    SCRATCH[_k] = ("sbuf", [128, M], BFD)
+for _k in ("FW", "NFW", "PFW", "EW"):
+    SCRATCH[_k] = ("sbuf", [128, 32], U16)
+for _k in ("NXW", "TWL", "PTW"):
+    SCRATCH[_k] = ("sbuf", [128, 256], U16)
+for _k in range(8):
+    SCRATCH["ps%d" % _k] = ("psum", [128, 512], F32)
+SEMAPHORES = ["vec", "act", "ten", "gps", "ldn", "ldp", "ldt", "ldf", "xa", "xb", "xc", "xd", "m2a", "m2b", "u20", "u21", "u22",
+              "u23", "lan1", "lan3", "rnl", "otn", "opt", "stn", "sty", "a1", "an", "a2", "s1", "sn", "s2"]
+ADD, SUB, MUL = AluOpType.add, AluOpType.subtract, AluOpType.mult
+IDN = ActivationFunctionType.Identity
+CHUNKS = [(0, 64), (64, 128), (128, 192), (192, 224), (224, 240), (240, 256)]
+
+
+def slot(r, q):
+    return q - (1 if q > r else 0)
+
+
+def rank_program(g, core, T, topo):
+    r = T.rank_of(core)
+    if r is None:
+        return
+    base = H * r
+    cores = T.cores
+    total, seen = {}, {}
+
+    def inc(op, s, n=1):
+        op.then_inc(T.sem[s], n)
+        total[s] = total.get(s, 0) + n
+        return (s, total[s])
+
+    def wait(qn, q, toks):
+        best = {}
+        for s, v in toks:
+            best[s] = max(best.get(s, 0), v)
+        for s in best:
+            if seen.get((qn, s), 0) < best[s]:
+                q.wait_ge(T.sem[s], best[s])
+                seen[(qn, s)] = best[s]
+
+    V, S, P, Y = g.vector, g.scalar, g.tensor, g.sync
+
+    def vec(f, *toks):
+        wait("v", V, toks)
+        return inc(f(), "vec")
+
+    def act(f, *toks):
+        wait("s", S, toks)
+        return inc(f(), "act")
+
+    def gps(f, *toks):
+        wait("g", g, toks)
+        return inc(f(), "gps")
+
+    def sdma(sem, out, in_, *toks):
+        wait("y", Y, toks)
+        return inc(Y.dma_start(out, in_), sem, 16)
+
+    def wrap(b, n, d, src, c0, *toks):
+        wait("t", P, toks)
+        tok = None
+        for p in range(16):
+            mm = P.matmul(T["ps%d" % b][:, 0:n], d[:, p, :], src[:, 16 * c0 + p:16 * (c0 + n):16], p == 0, p == 15)
+            if p == 15:
+                tok = inc(mm, "ten")
+        return tok
+
+    def evac(out, b, n, tok):
+        return vec(lambda: V.tensor_scalar(out, T["ps%d" % b][:, 0:n], float(base), None, SUB), tok)
+
+    def lane(t, k):
+        return t[k:128:16, 0:H]
+
+    def qd(t, k):
+        return t[:, 64 * k:64 * k + 64]
+
+    def rows(t, k):
+        return t[:, 1024 * k:1024 * k + 1024]
+
+    ldn = sdma("ldn", T.NA[:, :], T.nxt[:, :])
+    ldp = sdma("ldp", T.PA[:, :], T.prv[:, :])
+    ldf = inc(S.dma_start(T.FA[:, :], T.far[:, :]), "ldf", 16)
+    ldt = inc(S.dma_start(T.TA[:, :], T.twn[:, :]), "ldt", 16)
+    xa = sdma("xa", T.X[:, 0:2048], T.x[:, 0:2048])
+    xb = sdma("xb", T.X[:, 2048:H], T.x[:, 2048:H])
+
+    v_eq = vec(lambda: V.memset(T.EQ[:, :, :], 1.0))
+    v_bm = vec(lambda: V.memset(T.BM[:, :], 1.0))
+    v_nw = vec(lambda: V.memset(T.NW[:, 0:H], 0.0))
+    GE, IE = AluOpType.is_ge, AluOpType.is_equal
+    g_eq = gps(lambda: g.affine_select(T.EQ[:, :, :], T.EQ[:, :, :], [[1, 16], [-1, 16]], IE, 0.0, 0, 0), v_eq)
+    g_b1 = gps(lambda: g.affine_select(T.BM[:, :], T.BM[:, :], [[-2, 2], [-16, 8]], GE, 0.0, 0, 1), v_bm)
+    g_bm = gps(lambda: g.affine_select(T.BM[:, :], T.BM[:, :], [[2, 2], [16, 8]], GE, 0.0, 1, -1), g_b1)
+    g_li = gps(lambda: g.iota(T.LI[:, 0:1], [[0, 1]], 0, 1))
+
+    def iot(ap, pat, b):
+        return gps(lambda: g.iota(ap, pat, b, 0, allow_small_or_imprecise_dtypes=True))
+    iot(T.HI[:, :], [[256, 2], [0, 4]], base + H)
+    iot(T.OF[:, :], [[0, 2], [64, 4]], 0)
+    g_si = iot(T.SI[:, :], [[1, 64]], 0)
+    g_n3 = iot(T.N3[:, 0:2048], [[0, 2048]], 0)
+
+    def split(a, h, l, ld):
+        t = vec(lambda: V.tensor_copy(h[:, :], a[:, :]), ld)
+        return vec(lambda: V.tensor_tensor(l[:, :], a[:, :], h[:, :], SUB), t)
+    v_nl = split(T.NA, T.NH, T.NL, ldn)
+    v_pl = split(T.PA, T.PH, T.PL, ldp)
+    v_tl = split(T.TA, T.TH, T.TL, ldt)
+    v_fw = vec(lambda: V.tensor_copy(T.FW[:, 0:28], T.FA[:, :]), ldf)
+    v_la = vec(lambda: V.tensor_scalar(T.LA[:, 0:1], T.LI[:, 0:1], 15, None, AluOpType.bitwise_and), g_li)
+    v_l2 = vec(lambda: V.tensor_scalar(T.LM[:, 0:1], T.LA[:, 0:1], 2.0, None, IE), v_la)
+    v_l3 = vec(lambda: V.tensor_scalar(T.LM[:, 4:5], T.LA[:, 0:1], 3.0, None, IE), v_la)
+    v_h = vec(lambda: V.tensor_scalar(T.HI[:, :], T.HI[:, :], T.LM[:, 0:1], None, MUL), v_l2, g_si)
+    v_o = vec(lambda: V.tensor_scalar(T.OF[:, :], T.OF[:, :], T.LM[:, 4:5], None, MUL), v_l3, g_si)
+    v_bb = vec(lambda: V.tensor_tensor(T.BB[:, :], T.HI[:, :], T.OF[:, :], ADD), v_h, v_o)
+    v_n3 = vec(lambda: V.memset(T.N3[:, 2048:H], 0.0))
+    v_x0 = vec(lambda: V.tensor_scalar(T.NX[:, 0:1024:4], T.NA[:, :], 4.0, None, MUL), ldn)
+    v_x3 = vec(lambda: V.tensor_scalar(T.NX[:, 3:1024:4], T.PA[:, :], 4.0, 1.0, MUL, ADD), ldp)
+
+    sdma("lan1", lane(T.NW, 0), T.NH[:, :], v_nw, v_nl)
+    sdma("lan1", lane(T.NW, 1), T.NL[:, :])
+    for k in (2, 4):
+        sdma("lan1", lane(T.NW, k), T.PH[:, :], v_pl)
+        sdma("lan1", lane(T.NW, k + 1), T.PL[:, :])
+    sdma("lan1", lane(T.NW, 6), T.TH[:, :], v_tl)
+    lan1 = sdma("lan1", lane(T.NW, 7), T.TL[:, :])
+    sdma("lan3", lane(T.N3, 2), T.TH[:, :], v_n3, g_n3)
+    lan3 = sdma("lan3", lane(T.N3, 3), T.TL[:, :])
+    xc = sdma("xc", T.X2[:, 0:2048], T.x[:, 0:2048])
+    xd = sdma("xd", T.X2[:, 2048:H], T.x[:, 2048:H])
+
+    def build(u):
+        tok = None
+        d = T["D%d" % u]
+        for k in range(8):
+            tok = act(lambda: S.activation(d[:, :, 16 * k:16 * k + 16], T.EQ[:, :, :], IDN,
+                                           scale=T.BM[:, 8 * u + k:8 * u + k + 1]), g_eq, g_bm)
+        return tok
+    s_d0 = build(0)
+    s_d1 = build(1)
+    s_xf = act(lambda: S.activation(T.XF[:, :], T.X[:, :].indirect(T.FW[:, 0:28]), IDN), v_fw, xa, xb)
+    s_c3 = None
+    for i in range(NS):
+        s_c3 = act(lambda: S.activation(T.C3[:, E * i:E * i + E], T.SI[:, :], IDN, bias=T.BB[:, i:i + 1],
+                                        scale=T.LM[:, 4:5]), v_bb, g_si)
+    s_ce = act(lambda: S.activation(T.NW[:, H:HX], T.C3[:, :], IDN), s_c3)
+
+    v_r1 = vec(lambda: V.tensor_copy(T.R1[:, :], T.NW[:, 0:H].indirect(T.FW[:, 0:28])), lan1, v_fw)
+    t_nq = [wrap(0, 64, T.D0, T.NW, 0, lan1, s_d0)]
+    t_nf = wrap(1, 28, T.D0, T.R1, 0, v_r1)
+    t_nq += [wrap(3, 64, T.D0, T.NW, 64), wrap(4, 64, T.D0, T.NW, 128)]
+    t_pf = wrap(2, 28, T.D1, T.R1, 0, s_d1)
+    t_nq.append(wrap(5, 64, T.D0, T.NW, 192))
+    v_nq = [evac(qd(T.NXW, 0), 0, 64, t_nq[0])]
+    v_nf = evac(T.NFW[:, 0:28], 1, 28, t_nf)
+    v_mf = vec(lambda: V.tensor_tensor(T.MF[:, :], T.X[:, :].indirect(T.NFW[:, 0:28]), T.XF[:, :], ADD), v_nf, s_xf, xa, xb)
+    v_nq.append(evac(qd(T.NXW, 1), 3, 64, t_nq[1]))
+    v_c3 = vec(lambda: V.tensor_copy(T.N3[:, :].indirect(T.FW[:, 0:28]), T.C3[:, :]), lan3, s_c3)
+    v_nq.append(evac(qd(T.NXW, 2), 4, 64, t_nq[2]))
+    v_pf = evac(T.PFW[:, 0:28], 2, 28, t_pf)
+    v_ee = vec(lambda: V.tensor_copy(T.EE[:, :], T.N3[:, :].indirect(T.PFW[:, 0:28])), v_pf, v_c3)
+    v_nq.append(evac(qd(T.NXW, 3), 5, 64, t_nq[3]))
+    t_tw = [wrap(6, 64, T.D1, T.N3, 0, v_c3), wrap(7, 64, T.D1, T.N3, 64)]
+    t_e = wrap(1, 28, T.D1, T.EE, 0, v_ee, v_nf)
+    t_tw.append(wrap(0, 64, T.D1, T.N3, 128, v_nq[0]))
+    t_tw.append(wrap(2, 64, T.D1, T.N3, 192, v_pf))
+
+    def order():
+        used, plan = [], []
+        away = [q for q in range(8) if q != r and topo.chip(cores[q]) != topo.chip(core)]
+        near = [q for q in range(8) if q != r and topo.chip(cores[q]) == topo.chip(core)]
+        for q in away + near:
+            es = topo.engines(core, cores[q])
+            es = es[::2] + es[1::2]
+            e = [k for k in es if k not in used][0]
+            used.append(e)
+            plan.append((q, e))
+        return plan
+    plan = order()
+
+    def send(src, dst, d0, rs, ls, *toks):
+        wait("g", g, toks)
+        tr = []
+        for q, e in plan:
+            rid, pid, _se = topo.addr(cores[q])
+            i, k = slot(r, q), slot(q, r)
+            tr.append(RemoteDMATransfer(dst_ids=[DstId(rid=rid, pnc=pid)], dma_engine_mask=1 << e, remote_sem=T.sem[rs],
+                                        src=src[:, E * i:E * i + E], dst=dst[:, d0 + E * k:d0 + E * k + E]))
+        g.remote_dma_fused(tr, local_sem=T.sem[ls])
+        total[ls] = NS
+        total[rs] = NS
+    a1, an, a2 = ("a1", NS), ("an", NS), ("a2", NS)
+    send(T.R1, T.RN, 0, "an", "sn", v_r1)
+    send(T.MF, T.MX, H, "a1", "s1", v_mf)
+    sdma("rnl", T.NW[4:128:16, H:HX], T.RN[4:128:16, :], an, s_ce)
+    rnl = sdma("rnl", T.NW[5:128:16, H:HX], T.RN[5:128:16, :])
+
+    def m_pass(k):
+        return vec(lambda: V.tensor_tensor(rows(T.MX, k), T.X[:, :].indirect(qd(T.NXW, k)), rows(T.X2, k), ADD),
+                   v_nq[k], xa, xb, xc if k < 2 else xd)
+    v_m = [m_pass(0)]
+    v_tw = [evac(qd(T.TWL, 0), 6, 64, t_tw[0])]
+    v_m.append(m_pass(1))
+    m2a = sdma("m2a", T.M2[:, 0:2048], T.MX[:, 0:2048], v_m[1])
+    v_tw.append(evac(qd(T.TWL, 1), 7, 64, t_tw[1]))
+    v_m.append(m_pass(2))
+    v_e = evac(T.EW[:, 0:28], 1, 28, t_e)
+    v_tw.append(evac(qd(T.TWL, 2), 0, 64, t_tw[2]))
+    v_m.append(m_pass(3))
+    v_tw.append(evac(qd(T.TWL, 3), 2, 64, t_tw[3]))
+    m2b = sdma("m2b", T.M2[:, 2048:H], T.MX[:, 2048:H], v_m[3])
+
+    s_nn = None
+    for k in range(4):
+        s_nn = act(lambda: S.activation(rows(T.NN, k), T.NW[:, 0:H].indirect(qd(T.NXW, k)), IDN), lan1, v_nq[k])
+
+    def q_pass(h):
+        return vec(lambda: V.tensor_tensor(T.Q[:, 2048 * h:2048 * h + 2048], T.MX[:, 0:H].indirect(T.NXW[:, 128 * h:128 * h + 128]),
+                                           T.M2[:, 2048 * h:2048 * h + 2048], ADD), v_m[3], v_nq[3], (m2a, m2b)[h])
+    v_vv = vec(lambda: V.tensor_copy(T.VV[:, :], T.MX[:, :].indirect(T.EW[:, 0:28])), a1, v_m[3], v_e)
+    send(T.VV, T.UX, H, "a2", "s2", v_vv)
+    v_qa = q_pass(0)
+    v_qb = q_pass(1)
+
+    s_nt, t_pt = [], []
+    free = [v_nq[1], v_nq[2], v_nq[3], v_tw[0]]
+    for k in range(4):
+        s_nt.append(act(lambda: S.activation(rows(T.NT, k), T.NW[:, :].indirect(qd(T.TWL, k)), IDN), rnl, s_ce, v_tw[k]))
+        t_pt.append(wrap(3 + k, 64, T.D1, T.NT, 64 * k, s_nt[k], free[k]))
+
+    sdma("otn", T.TNH[:, :], lane(T.NN, 6), s_nn)
+    otn = sdma("otn", T.TNL[:, :], lane(T.NN, 7))
+    sdma("opt", T.PTH[:, :], lane(T.NT, 4), s_nt[3])
+    opt = sdma("opt", T.PTL[:, :], lane(T.NT, 5))
+
+    u, u2 = [], []
+    for k in range(4):
+        u.append(act(lambda: S.activation(rows(T.UX, k), T.MX[:, :].indirect(qd(T.TWL, k)), IDN), a1, v_m[3], v_tw[k]))
+        u2.append(sdma("u2%d" % k, rows(T.U2, k), rows(T.UX, k), u[k]))
+
+    v_t1 = vec(lambda: V.tensor_tensor(T.TMP[:, :], T.TNH[:, :], T.TNL[:, :], ADD), otn)
+    v_x1 = vec(lambda: V.tensor_scalar(T.NX[:, 1:1024:4], T.TMP[:, :], 4.0, 3.0, MUL, ADD), v_t1)
+    v_pt = [evac(qd(T.PTW, k), 3 + k, 64, t_pt[k]) for k in range(4)]
+    v_t2 = vec(lambda: V.tensor_tensor(T.TMP2[:, :], T.PTH[:, :], T.PTL[:, :], ADD), opt)
+    v_x2 = vec(lambda: V.tensor_scalar(T.NX[:, 2:1024:4], T.TMP2[:, :], 4.0, 2.0, MUL, ADD), v_t2)
+    sdma("stn", T.nx[:, :], T.NX[:, :], v_x0, v_x1, v_x2, v_x3)
+
+    for a, b in CHUNKS:
+        s_ye = act(lambda: S.activation(T.Y[:, 32 * a:32 * b:2], T.Q[:, :].indirect(T.NXW[:, a:b]), IDN), v_qa, v_qb)
+        v_yo = vec(lambda: V.tensor_tensor(T.Y[:, 32 * a + 1:32 * b:2], T.UX[:, :].indirect(T.PTW[:, a:b]), T.U2[:, 16 * a:16 * b],
+                                           ADD), a2, u2[a // 64], v_pt[a // 64], *u)
+        sdma("sty", T.y[:, 32 * a:32 * b], T.Y[:, 32 * a:32 * b], s_ye, v_yo)
+
+    wait("g", g, [(s, total[s]) for s in total])

@@ -5,41 +5,54 @@ H, E, NS = 4096, 64, 7
 M = NS * E
 HX = H + M
 BFD, F32, I32, U16 = "bfloat16", "float32", "int32", "uint16"
-SCRATCH = {"NX": ("sbuf", [128, 1024], F32), "EQ": ("sbuf", [128, 16, 16], BFD), "BM": ("sbuf", [128, 16], F32),
-           "Y": ("sbuf", [128, 2 * H], BFD), "FA": ("sbuf", [128, 28], I32), "SI": ("sbuf", [128, 64], F32)}
-for _k in ("X", "X2", "M2", "U2", "N3", "NN", "NT", "Q"):
+SCRATCH = {"NX": ("sbuf", [128, 2, 128, 4], F32), "Y": ("sbuf", [128, 2 * H], BFD), "FA": ("sbuf", [128, 28], I32),
+           "N0": ("sbuf", [128, 2, 2, 128], I32), "NF": ("sbuf", [128, 8, 32], F32), "NG": ("sbuf", [128, 256], F32),
+           "NA": ("sbuf", [128, 3, 256], I32), "NH": ("sbuf", [128, 3, 256], BFD), "NL": ("sbuf", [128, 3, 256], BFD),
+           "D": ("sbuf", [128, 4, 144], BFD), "BM": ("sbuf", [128, 4, 8], BFD), "LO": ("sbuf", [128, M], F32),
+           "ID": ("sbuf", [128, 128], BFD), "NO": ("sbuf", [128, 4, 2, 128], BFD)}
+for _k in ("X", "X2", "M1", "NN", "NT"):
     SCRATCH[_k] = ("sbuf", [128, H], BFD)
-for _k in ("NW", "MX", "UX"):
+for _k in ("NW", "MX", "RX"):
     SCRATCH[_k] = ("sbuf", [128, HX], BFD)
-for _k in ("NA", "PA", "TA"):
-    SCRATCH[_k] = ("sbuf", [128, 256], I32)
-for _k in ("NH", "NL", "PH", "PL", "TH", "TL", "TNH", "TNL", "PTH", "PTL"):
-    SCRATCH[_k] = ("sbuf", [128, 256], BFD)
-for _k in ("TMP", "TMP2"):
-    SCRATCH[_k] = ("sbuf", [128, 256], F32)
-for _k in ("D0", "D1"):
-    SCRATCH[_k] = ("sbuf", [128, 16, 128], BFD)
 for _k in ("LI", "LA"):
-    SCRATCH[_k] = ("sbuf", [128, 8], I32)
-for _k in ("LM", "HI", "OF", "BB"):
-    SCRATCH[_k] = ("sbuf", [128, 8], F32)
+    SCRATCH[_k] = ("sbuf", [128, 4], I32)
+for _k in ("LM", "HB", "KP"):
+    SCRATCH[_k] = ("sbuf", [128, 4], F32)
 for _k in ("C3", "R1", "RN", "XF", "MF", "EE", "VV"):
     SCRATCH[_k] = ("sbuf", [128, M], BFD)
 for _k in ("FW", "NFW", "PFW", "EW"):
     SCRATCH[_k] = ("sbuf", [128, 32], U16)
-for _k in ("NXW", "TWL", "PTW"):
+for _k in ("NXW", "N2W", "TWL", "PTW"):
     SCRATCH[_k] = ("sbuf", [128, 256], U16)
 for _k in range(8):
     SCRATCH["ps%d" % _k] = ("psum", [128, 512], F32)
-SEMAPHORES = ["vec", "act", "ten", "gps", "ldn", "ldp", "ldt", "ldf", "xa", "xb", "xc", "xd", "m2a", "m2b", "u20", "u21", "u22",
-              "u23", "lan1", "lan3", "rnl", "otn", "opt", "stn", "sty", "a1", "an", "a2", "s1", "sn", "s2"]
+SEMAPHORES = ["vec", "act", "ten", "gps", "ldb", "ldt", "ldp", "ld0", "ldf", "x0", "x1", "x2", "x3", "xc", "xm", "o0", "o1", "o2", "o3",
+              "lan", "rnl", "stn", "sty", "a1", "an", "a2", "s1", "sn", "s2"]
 ADD, SUB, MUL = AluOpType.add, AluOpType.subtract, AluOpType.mult
+GE, IE = AluOpType.is_ge, AluOpType.is_equal
 IDN = ActivationFunctionType.Identity
-CHUNKS = [(0, 64), (64, 128), (128, 192), (192, 224), (224, 240), (240, 256)]
+NEXT, PREV, CODE = 0, 1, 3
+LOW = {1: 1, 4: 0}
+PNUM, TWIN = 4, 8
+
+VECTOR = ("m 0 128, m 128 256, mf, nn 200 256, pf_list, codes, n2_list 0 192, n2_list 192 256, nx0, ye 0 72, e_list, tw_list 0 64, "
+          "nx3, vv, tw_list 64 160, r 0 56, tw_list 160 256, r 56 136, pt_list 0 64, r 136 200, r 200 256, pt_list 64 128, "
+          "pt_list 128 192, ye 72 128, yo 104 144, pt_list 192 256, ye 128 192, ye 192 232, ye 232 256")
+SCALAR = ("x2 0 64, x2 64 128, x2 128 192, r1, nn 0 64, nn 64 128, nn 128 200, m1 0 72, m1 72 152, ee, m1 152 256, nt 0 64, nt 64 128, "
+          "nt 128 192, nt 192 256, nx1, nx2 0 128, yo 0 32, yo 32 72, yo 72 104, nx2 128 256, yo 144 192, yo 192 232, yo 232 256")
+TENSOR = ("pf, n2 0 64, n2 64 128, n2 128 192, n2 192 256, tw 0 64, e, tw 64 160, tw 160 256, tn 0 128, tn 128 256, "
+          "pt 0 64, pt 64 128, pt 128 192, pn 0 128, pt 192 256, pn 128 256")
+GPSIMD = "send_numbers, send_m, send_r"
+SYNC = ("x2 192 256, old_numbers, tn_out 0 128, tn_out 128 256, numbers_in, pn_out 0 128, pn_out 128 256, nx 0 128, y 0 32, y 32 72, "
+        "y 72 128, nx 128 256, y 128 192, y 192 232, y 232 256")
 
 
 def slot(r, q):
     return q - (1 if q > r else 0)
+
+
+def steps(text):
+    return [(w[0], int(w[1]), int(w[2])) if len(w) > 1 else (w[0], 0, 256) for w in (s.split() for s in text.split(","))]
 
 
 def rank_program(g, core, T, topo):
@@ -82,114 +95,113 @@ def rank_program(g, core, T, topo):
         wait("y", Y, toks)
         return inc(Y.dma_start(out, in_), sem, 16)
 
-    def wrap(b, n, d, src, c0, *toks):
+    def ps(b, n, at=0):
+        return T["ps%d" % b][:, at:at + n]
+
+    def wrap(b, n, u, src, c0, *toks, at=0):
         wait("t", P, toks)
-        tok = None
         for p in range(16):
-            mm = P.matmul(T["ps%d" % b][:, 0:n], d[:, p, :], src[:, 16 * c0 + p:16 * (c0 + n):16], p == 0, p == 15)
-            if p == 15:
-                tok = inc(mm, "ten")
+            mm = P.matmul(ps(b, n, at), T.D[:, u, 15 - p:143 - p], src[:, 16 * c0 + p:16 * (c0 + n):16], p == 0, p == 15)
+        return inc(mm, "ten")
+
+    def pair_out(j, src, k, a, b, *toks):
+        for d in range(2):
+            tok = sdma("o%d" % j, T.NO[:, j, d], src[k + d:128:16, 16 * a:16 * b], *toks)
         return tok
 
-    def evac(out, b, n, tok):
-        return vec(lambda: V.tensor_scalar(out, T["ps%d" % b][:, 0:n], float(base), None, SUB), tok)
+    def pair_sum(b, at, j, *toks):
+        wait("t", P, toks)
+        for d in range(2):
+            mm = P.matmul(ps(b, 128, at), T.ID[:, :], T.NO[:, j, d], d == 0, d == 1)
+        return inc(mm, "ten")
+
+    def evac(out, src, *toks):
+        return vec(lambda: V.tensor_scalar(out, src, float(base), None, SUB), *toks)
 
     def lane(t, k):
         return t[k:128:16, 0:H]
 
-    def qd(t, k):
-        return t[:, 64 * k:64 * k + 64]
-
     def rows(t, k):
         return t[:, 1024 * k:1024 * k + 1024]
 
-    ldn = sdma("ldn", T.NA[:, :], T.nxt[:, :])
-    ldp = sdma("ldp", T.PA[:, :], T.prv[:, :])
+    def cols(t, a, b):
+        return t[:, 16 * a:16 * b]
+
+    def take(q, out, win, lst, *toks):
+        if q == "v":
+            return vec(lambda: V.tensor_copy(out, win.indirect(lst)), *toks)
+        return act(lambda: S.activation(out, win.indirect(lst), IDN), *toks)
+
+    def vsum(out, win, lst, in1, *toks):
+        return vec(lambda: V.tensor_tensor(out, win.indirect(lst), in1, ADD), *toks)
+
+    far = T.FW[:, 0:28]
+    X, MX, ML, NW, NWL = T.X[:, :], T.MX[:, :], T.MX[:, 0:H], T.NW[:, :], T.NW[:, 0:H]
+
+    ldt = sdma("ldt", T.NA[:, 2], T.twn[:, :])
+    inc(S.dma_start(T.NA[:, 0, 0:128], T.nxt[0:8:2, :]), "ldb", 16)
+    ldb = sdma("ldb", T.NA[:, 0, 128:256], T.nxt[1:8:2, :])
+    ldp = inc(S.dma_start(T.NA[:, 1], T.prv[:, :]), "ldp", 16)
     ldf = inc(S.dma_start(T.FA[:, :], T.far[:, :]), "ldf", 16)
-    ldt = inc(S.dma_start(T.TA[:, :], T.twn[:, :]), "ldt", 16)
-    xa = sdma("xa", T.X[:, 0:2048], T.x[:, 0:2048])
-    xb = sdma("xb", T.X[:, 2048:H], T.x[:, 2048:H])
+    xs = [sdma("x%d" % k, rows(T.X, k), rows(T.x, k)) for k in range(4)]
 
-    v_eq = vec(lambda: V.memset(T.EQ[:, :, :], 1.0))
-    v_bm = vec(lambda: V.memset(T.BM[:, :], 1.0))
-    v_nw = vec(lambda: V.memset(T.NW[:, 0:H], 0.0))
-    GE, IE = AluOpType.is_ge, AluOpType.is_equal
-    g_eq = gps(lambda: g.affine_select(T.EQ[:, :, :], T.EQ[:, :, :], [[1, 16], [-1, 16]], IE, 0.0, 0, 0), v_eq)
-    g_b1 = gps(lambda: g.affine_select(T.BM[:, :], T.BM[:, :], [[-2, 2], [-16, 8]], GE, 0.0, 0, 1), v_bm)
-    g_bm = gps(lambda: g.affine_select(T.BM[:, :], T.BM[:, :], [[2, 2], [16, 8]], GE, 0.0, 1, -1), g_b1)
-    g_li = gps(lambda: g.iota(T.LI[:, 0:1], [[0, 1]], 0, 1))
+    def iot(ap, pat, b, *toks):
+        return gps(lambda: g.iota(ap, pat, b, 0, allow_small_or_imprecise_dtypes=True), *toks)
 
-    def iot(ap, pat, b):
-        return gps(lambda: g.iota(ap, pat, b, 0, allow_small_or_imprecise_dtypes=True))
-    iot(T.HI[:, :], [[256, 2], [0, 4]], base + H)
-    iot(T.OF[:, :], [[0, 2], [64, 4]], 0)
-    g_si = iot(T.SI[:, :], [[1, 64]], 0)
-    g_n3 = iot(T.N3[:, 0:2048], [[0, 2048]], 0)
+    g_li = gps(lambda: g.iota(T.LI[:, :], [[-8, 2], [-1, 2]], 14, 1))
+    g_lo = iot(T.LO[:, :], [[1, M]], -256)
+    g_one = iot(T.BM[:, :, :], [[0, 32]], 1)
+    g_b = gps(lambda: g.affine_select(T.BM[:, :, :], T.BM[:, :, :], [[-8, 2], [-2, 2], [-16, 8]], GE, 0.0, 0, 1), g_one)
+    g_hi = {k: gps(lambda: g.affine_select(T.NH[:, k], T.NA[:, k], [[0, 256]], GE, 0.0, 0, 0), ld) for k, ld in ((2, ldt), (1, ldp), (0, ldb))}
 
-    def split(a, h, l, ld):
-        t = vec(lambda: V.tensor_copy(h[:, :], a[:, :]), ld)
-        return vec(lambda: V.tensor_tensor(l[:, :], a[:, :], h[:, :], SUB), t)
-    v_nl = split(T.NA, T.NH, T.NL, ldn)
-    v_pl = split(T.PA, T.PH, T.PL, ldp)
-    v_tl = split(T.TA, T.TH, T.TL, ldt)
-    v_fw = vec(lambda: V.tensor_copy(T.FW[:, 0:28], T.FA[:, :]), ldf)
-    v_la = vec(lambda: V.tensor_scalar(T.LA[:, 0:1], T.LI[:, 0:1], 15, None, AluOpType.bitwise_and), g_li)
-    v_l2 = vec(lambda: V.tensor_scalar(T.LM[:, 0:1], T.LA[:, 0:1], 2.0, None, IE), v_la)
-    v_l3 = vec(lambda: V.tensor_scalar(T.LM[:, 4:5], T.LA[:, 0:1], 3.0, None, IE), v_la)
-    v_h = vec(lambda: V.tensor_scalar(T.HI[:, :], T.HI[:, :], T.LM[:, 0:1], None, MUL), v_l2, g_si)
-    v_o = vec(lambda: V.tensor_scalar(T.OF[:, :], T.OF[:, :], T.LM[:, 4:5], None, MUL), v_l3, g_si)
-    v_bb = vec(lambda: V.tensor_tensor(T.BB[:, :], T.HI[:, :], T.OF[:, :], ADD), v_h, v_o)
-    v_n3 = vec(lambda: V.memset(T.N3[:, 2048:H], 0.0))
-    v_x0 = vec(lambda: V.tensor_scalar(T.NX[:, 0:1024:4], T.NA[:, :], 4.0, None, MUL), ldn)
-    v_x3 = vec(lambda: V.tensor_scalar(T.NX[:, 3:1024:4], T.PA[:, :], 4.0, 1.0, MUL, ADD), ldp)
+    v_nw = vec(lambda: V.memset(T.NW[:, 0:1024], 0.0))
+    vec(lambda: V.memset(T.NW[:, 1024:3072], 0.0))
+    v_la = vec(lambda: V.tensor_scalar(T.LA[:, :], T.LI[:, :], 15, None, AluOpType.bitwise_and), g_li)
+    vec(lambda: V.tensor_scalar(T.LM[:, :], T.LA[:, :], 0.0, None, IE), v_la)
+    vec(lambda: V.tensor_scalar(T.KP[:, 0:1], T.LA[:, 2:3], 2.0, None, GE))
+    v_hb = vec(lambda: V.tensor_scalar(T.HB[:, :], T.LA[:, :], 0.0, float(base + H + 256), IE, MUL))
 
-    sdma("lan1", lane(T.NW, 0), T.NH[:, :], v_nw, v_nl)
-    sdma("lan1", lane(T.NW, 1), T.NL[:, :])
-    for k in (2, 4):
-        sdma("lan1", lane(T.NW, k), T.PH[:, :], v_pl)
-        sdma("lan1", lane(T.NW, k + 1), T.PL[:, :])
-    sdma("lan1", lane(T.NW, 6), T.TH[:, :], v_tl)
-    lan1 = sdma("lan1", lane(T.NW, 7), T.TL[:, :])
-    sdma("lan3", lane(T.N3, 2), T.TH[:, :], v_n3, g_n3)
-    lan3 = sdma("lan3", lane(T.N3, 3), T.TL[:, :])
-    xc = sdma("xc", T.X2[:, 0:2048], T.x[:, 0:2048])
-    xd = sdma("xd", T.X2[:, 2048:H], T.x[:, 2048:H])
+    act(lambda: S.activation(T.NW[:, 3072:H], T.NW[:, 0:1024], IDN), v_nw)
+    s_d0 = act(lambda: S.activation(T.D[:, :, :], T.NW[:, 0:576], IDN))
+    s_c3 = act(lambda: S.activation(T.C3[:, :], T.LO[:, :], IDN, bias=T.HB[:, 2:3], scale=T.LM[:, 3:4]), v_hb, g_lo)
+    s_ce = act(lambda: S.activation(T.NW[:, H:HX], T.LO[:, :], IDN, bias=T.HB[:, 0:1], scale=T.LM[:, 1:2]))
+    g_d = gps(lambda: g.affine_select(T.D[:, :, 15:128:16], T.BM[:, :, :], [[8, 2], [2, 2], [16, 8]], GE, 0.0, 1, -1), g_b, s_d0)
+    g_i1 = iot(T.ID[:, :], [[0, 128]], 1)
+    g_id = gps(lambda: g.affine_select(T.ID[:, :], T.ID[:, :], [[-1, 128]], IE, 0.0, 0, 1), g_i1)
 
-    def build(u):
-        tok = None
-        d = T["D%d" % u]
-        for k in range(8):
-            tok = act(lambda: S.activation(d[:, :, 16 * k:16 * k + 16], T.EQ[:, :, :], IDN,
-                                           scale=T.BM[:, 8 * u + k:8 * u + k + 1]), g_eq, g_bm)
+    def low(k):
+        return vec(lambda: V.tensor_tensor(T.NL[:, k], T.NA[:, k], T.NH[:, k], SUB), g_hi[k])
+    for e in range(2):
+        v_f = vec(lambda: V.tensor_scalar(T.NF[:, :, 16 * e:16 * e + 16], T.NA[:, 0, 128 * e:128 * e + 128], float(base), None, SUB), ldb)
+    v_lo = {2: low(2)}
+    v_fw = vec(lambda: V.tensor_copy(far, T.FA[:, :]), ldf)
+    for b in range(8):
+        v_g = vec(lambda: V.transpose(T.NG[:, b:256:8], T.NF[:, b, :]), v_f)
+        if b in LOW:
+            v_lo[LOW[b]] = low(LOW[b])
+    v_nq = vec(lambda: V.tensor_copy(T.NXW[:, :], T.NG[:, :]), v_g)
+    for j, ks in ((2, (TWIN, 10)), (1, (2, PNUM)), (0, ())):
+        for d, t, tok in ((0, T.NH, g_hi[j]), (1, T.NL, v_lo[j])):
+            if j == 0:
+                for e in range(2):
+                    lan = sdma("lan", T.NW[16 * e + d:128:32, 0:H], t[:, 0, 128 * e:128 * e + 128], tok)
+            for k in ks:
+                sdma("lan", lane(T.NW, k + d), t[:, j], tok, s_d0, v_hb)
+
+    def second_x(q, a, b):
+        if q == "y":
+            return sdma("xc", cols(T.X2, a, b), cols(T.x, a, b))
+        return act(lambda: S.activation(cols(T.X2, a, b), cols(T.X, a, b), IDN), *xs[a // 64:(b - 1) // 64 + 1])
+
+    def add_x(a, b, *toks):
+        wait("g", g, toks)
+        return inc(g.dma_start(cols(T.MX, a, b), cols(T.x, a, b), accum_op=ADD), "xm", 16)
+
+    def old_numbers():
+        for j, t in enumerate((T.nxt, T.prv)):
+            for h in range(2):
+                tok = sdma("ld0", T.N0[:, j, h], t[:, 2048 * h:2048 * h + 2048])
         return tok
-    s_d0 = build(0)
-    s_d1 = build(1)
-    s_xf = act(lambda: S.activation(T.XF[:, :], T.X[:, :].indirect(T.FW[:, 0:28]), IDN), v_fw, xa, xb)
-    s_c3 = None
-    for i in range(NS):
-        s_c3 = act(lambda: S.activation(T.C3[:, E * i:E * i + E], T.SI[:, :], IDN, bias=T.BB[:, i:i + 1],
-                                        scale=T.LM[:, 4:5]), v_bb, g_si)
-    s_ce = act(lambda: S.activation(T.NW[:, H:HX], T.C3[:, :], IDN), s_c3)
-
-    v_r1 = vec(lambda: V.tensor_copy(T.R1[:, :], T.NW[:, 0:H].indirect(T.FW[:, 0:28])), lan1, v_fw)
-    t_nq = [wrap(0, 64, T.D0, T.NW, 0, lan1, s_d0)]
-    t_nf = wrap(1, 28, T.D0, T.R1, 0, v_r1)
-    t_nq += [wrap(3, 64, T.D0, T.NW, 64), wrap(4, 64, T.D0, T.NW, 128)]
-    t_pf = wrap(2, 28, T.D1, T.R1, 0, s_d1)
-    t_nq.append(wrap(5, 64, T.D0, T.NW, 192))
-    v_nq = [evac(qd(T.NXW, 0), 0, 64, t_nq[0])]
-    v_nf = evac(T.NFW[:, 0:28], 1, 28, t_nf)
-    v_mf = vec(lambda: V.tensor_tensor(T.MF[:, :], T.X[:, :].indirect(T.NFW[:, 0:28]), T.XF[:, :], ADD), v_nf, s_xf, xa, xb)
-    v_nq.append(evac(qd(T.NXW, 1), 3, 64, t_nq[1]))
-    v_c3 = vec(lambda: V.tensor_copy(T.N3[:, :].indirect(T.FW[:, 0:28]), T.C3[:, :]), lan3, s_c3)
-    v_nq.append(evac(qd(T.NXW, 2), 4, 64, t_nq[2]))
-    v_pf = evac(T.PFW[:, 0:28], 2, 28, t_pf)
-    v_ee = vec(lambda: V.tensor_copy(T.EE[:, :], T.N3[:, :].indirect(T.PFW[:, 0:28])), v_pf, v_c3)
-    v_nq.append(evac(qd(T.NXW, 3), 5, 64, t_nq[3]))
-    t_tw = [wrap(6, 64, T.D1, T.N3, 0, v_c3), wrap(7, 64, T.D1, T.N3, 64)]
-    t_e = wrap(1, 28, T.D1, T.EE, 0, v_ee, v_nf)
-    t_tw.append(wrap(0, 64, T.D1, T.N3, 128, v_nq[0]))
-    t_tw.append(wrap(2, 64, T.D1, T.N3, 192, v_pf))
 
     def order():
         used, plan = [], []
@@ -215,66 +227,78 @@ def rank_program(g, core, T, topo):
         g.remote_dma_fused(tr, local_sem=T.sem[ls])
         total[ls] = NS
         total[rs] = NS
+        return (ls, NS)
     a1, an, a2 = ("a1", NS), ("an", NS), ("a2", NS)
-    send(T.R1, T.RN, 0, "an", "sn", v_r1)
-    send(T.MF, T.MX, H, "a1", "s1", v_mf)
-    sdma("rnl", T.NW[4:128:16, H:HX], T.RN[4:128:16, :], an, s_ce)
-    rnl = sdma("rnl", T.NW[5:128:16, H:HX], T.RN[5:128:16, :])
 
-    def m_pass(k):
-        return vec(lambda: V.tensor_tensor(rows(T.MX, k), T.X[:, :].indirect(qd(T.NXW, k)), rows(T.X2, k), ADD),
-                   v_nq[k], xa, xb, xc if k < 2 else xd)
-    v_m = [m_pass(0)]
-    v_tw = [evac(qd(T.TWL, 0), 6, 64, t_tw[0])]
-    v_m.append(m_pass(1))
-    m2a = sdma("m2a", T.M2[:, 0:2048], T.MX[:, 0:2048], v_m[1])
-    v_tw.append(evac(qd(T.TWL, 1), 7, 64, t_tw[1]))
-    v_m.append(m_pass(2))
-    v_e = evac(T.EW[:, 0:28], 1, 28, t_e)
-    v_tw.append(evac(qd(T.TWL, 2), 0, 64, t_tw[2]))
-    v_m.append(m_pass(3))
-    v_tw.append(evac(qd(T.TWL, 3), 2, 64, t_tw[3]))
-    m2b = sdma("m2b", T.M2[:, 2048:H], T.MX[:, 2048:H], v_m[3])
+    def numbers_in():
+        sdma("rnl", T.NW[PNUM:128:16, H:HX], T.RN[2:128:16, :], an, s_ce)
+        return sdma("rnl", T.NW[PNUM + 1:128:16, H:HX], T.RN[3:128:16, :])
 
-    s_nn = None
-    for k in range(4):
-        s_nn = act(lambda: S.activation(rows(T.NN, k), T.NW[:, 0:H].indirect(qd(T.NXW, k)), IDN), lan1, v_nq[k])
+    queues = {"v": steps(VECTOR), "s": steps(SCALAR), "t": steps(TENSOR), "g": steps(GPSIMD), "y": steps(SYNC)}
+    every = [s for q in queues for s in queues[q]]
+    tw_bank = dict(zip([s[1] for s in queues["t"] if s[0] == "tw"], (2, 3, 7)))
+    pt_bank = {0: (1, "pf_list*"), 64: (2, "tw_list*"), 128: (3, "tw_list*"), 192: (4, "n2_list*")}
+    pn_bank = {0: (5, "n2_list*"), 128: (7, "tw_list*")}
 
-    def q_pass(h):
-        return vec(lambda: V.tensor_tensor(T.Q[:, 2048 * h:2048 * h + 2048], T.MX[:, 0:H].indirect(T.NXW[:, 128 * h:128 * h + 128]),
-                                           T.M2[:, 2048 * h:2048 * h + 2048], ADD), v_m[3], v_nq[3], (m2a, m2b)[h])
-    v_vv = vec(lambda: V.tensor_copy(T.VV[:, :], T.MX[:, :].indirect(T.EW[:, 0:28])), a1, v_m[3], v_e)
-    send(T.VV, T.UX, H, "a2", "s2", v_vv)
-    v_qa = q_pass(0)
-    v_qb = q_pass(1)
+    def n2_bank(a):
+        return (4, a) if a < 192 else (5, 0)
+    nxt_list, tw_list = (lambda a, b: T.NXW[:, a:b]), (lambda a, b: T.TWL[:, a:b])
+    STEP = {
+        "x2": ((), lambda q, a, b, t: second_x(q, a, b)),
+        "x1": ((), lambda q, a, b, t: take(q, cols(T.MX, a, b), X, nxt_list(a, b), v_nq, *xs)),
+        "m": (("x2", "x1"), lambda q, a, b, t: vsum(cols(T.MX, a, b), X, nxt_list(a, b), cols(T.X2, a, b), v_nq, *xs, *t) if q == "v"
+              else add_x(a, b, *t)),
+        "old_numbers": ((), lambda q, a, b, t: old_numbers()),
+        "r1": ((), lambda q, a, b, t: act(lambda: S.activation(T.R1[:, :], NWL.indirect(far), IDN, scale=T.KP[:, 0:1]), lan, v_fw)),
+        "nn": ((), lambda q, a, b, t: take(q, cols(T.NN, a, b), NWL, nxt_list(a, b), lan, v_nq)),
+        "mf": (("m",), lambda q, a, b, t: take(q, T.MF[:, :], ML, far, *t)),
+        "xf": ((), lambda q, a, b, t: take(q, T.XF[:, :], X, far, v_fw, *xs)),
+        "mf_early": (("xf", "nf_list"), lambda q, a, b, t: vsum(T.MF[:, :], X, T.NFW[:, 0:28], T.XF[:, :], *t)),
+        "codes": (("r1", "nn"), lambda q, a, b, t: vec(lambda: V.tensor_tensor(NWL.indirect(far), T.R1[:, :], T.C3[:, :], ADD), s_c3, *t)),
+        "m1": (("m*",), lambda q, a, b, t: take(q, cols(T.M1, a, b), ML, nxt_list(a, b), *t)),
+        "ee": (("pf_list", "codes"), lambda q, a, b, t: take(q, T.EE[:, :], NWL, T.PFW[:, 0:28], *t)),
+        "vv": (("e_list", "mf", "mf_early", "m"), lambda q, a, b, t: vsum(T.VV[:, :], MX, T.EW[:, 0:28], T.MF[:, :], a1, *t)),
+        "ye": (("m1", "n2_list"), lambda q, a, b, t: vsum(T.Y[:, 32 * a:32 * b:2], ML, T.N2W[:, a:b], cols(T.M1, a, b), *t)),
+        "r": (("m1", "tw_list"), lambda q, a, b, t: vsum(cols(T.RX, a, b), MX, tw_list(a, b), cols(T.M1, a, b), a1, *t)),
+        "nt": (("tw_list", "numbers_in"), lambda q, a, b, t: take(q, cols(T.NT, a, b), NW, tw_list(a, b), *t)),
+        "yo": (("r*", "pt_list"), lambda q, a, b, t: take(q, T.Y[:, 32 * a + 1:32 * b:2], T.RX[:, :], T.PTW[:, a:b], a2, *t)),
+        "nx0": (("old_numbers",), lambda q, a, b, t: vec(lambda: V.tensor_scalar(T.NX[:, :, :, 0], T.N0[:, 0], 4.0, None, MUL), *t)),
+        "nx3": (("old_numbers",), lambda q, a, b, t: vec(lambda: V.tensor_scalar(T.NX[:, :, :, 3], T.N0[:, 1], 4.0, 1.0, MUL, ADD), *t)),
+        "nx1": (("tn",), lambda q, a, b, t: act(lambda: S.activation(T.NX[:, :, :, 1], ps(0, 256), IDN, bias=3.0, scale=4.0), *t)),
+        "nx2": (("pn",), lambda q, a, b, t: act(lambda: S.activation(T.NX[:, a // 128, :, 2], ps(pn_bank[a][0], 128), IDN,
+                                                                     bias=2.0, scale=4.0), *t)),
+        "nf": (("r1",), lambda q, a, b, t: wrap(6, 28, NEXT, T.R1, 0, g_d, *t)),
+        "pf": (("r1",), lambda q, a, b, t: wrap(1, 28, PREV, T.R1, 0, g_d, *t)),
+        "e": (("ee", "nf_list"), lambda q, a, b, t: wrap(6, 28, CODE, T.EE, 0, *t)),
+        "n2": (("nn",), lambda q, a, b, t: wrap(n2_bank(a)[0], b - a, NEXT, T.NN, a, *t, at=n2_bank(a)[1])),
+        "tw": (("codes",), lambda q, a, b, t: wrap(tw_bank[a], b - a, CODE, T.NW, a, *t)),
+        "pt": (("nt",), lambda q, a, b, t: wrap(pt_bank[a][0], b - a, PREV, T.NT, a, *t)),
+        "tn": (("tn_out",), lambda q, a, b, t: pair_sum(0, a, a // 128, g_id, *t)),
+        "pn": (("pn_out",), lambda q, a, b, t: pair_sum(pn_bank[a][0], 0, 2 + a // 128, *t)),
+        "nf_list": (("nf",), lambda q, a, b, t: evac(T.NFW[:, 0:28], ps(6, 28), *t)),
+        "pf_list": (("pf",), lambda q, a, b, t: evac(T.PFW[:, 0:28], ps(1, 28), *t)),
+        "e_list": (("e",), lambda q, a, b, t: evac(T.EW[:, 0:28], ps(6, 28), *t)),
+        "n2_list": (("n2",), lambda q, a, b, t: evac(T.N2W[:, a:b], ps(n2_bank(a)[0], b - a), *t)),
+        "tw_list": (("tw",), lambda q, a, b, t: evac(T.TWL[:, a:b], ps(tw_bank[a], b - a), *t)),
+        "pt_list": (("pt",), lambda q, a, b, t: evac(T.PTW[:, a:b], ps(pt_bank[a][0], b - a), *t)),
+        "send_numbers": (("r1",), lambda q, a, b, t: send(T.R1, T.RN, 0, "an", "sn", *t)),
+        "send_m": (("mf", "mf_early"), lambda q, a, b, t: send(T.MF, T.MX, H, "a1", "s1", *t)),
+        "send_r": (("vv",), lambda q, a, b, t: send(T.VV, T.RX, H, "a2", "s2", *t)),
+        "numbers_in": ((), lambda q, a, b, t: numbers_in()),
+        "tn_out": (("nn",), lambda q, a, b, t: pair_out(a // 128, T.NN, TWIN, a, b, *t)),
+        "pn_out": (("nt",), lambda q, a, b, t: pair_out(2 + a // 128, T.NT, PNUM, a, b, *t)),
+        "y": (("ye", "yo"), lambda q, a, b, t: sdma("sty", T.y[:, 32 * a:32 * b], T.Y[:, 32 * a:32 * b], *t)),
+        "nx": (("nx0", "nx1", "nx2", "nx3"), lambda q, a, b, t: sdma("stn", T.nx[:, 64 * a:64 * b], T.NX[:, a // 128], *t)),
+    }
+    done = {}
 
-    s_nt, t_pt = [], []
-    free = [v_nq[1], v_nq[2], v_nq[3], v_tw[0]]
-    for k in range(4):
-        s_nt.append(act(lambda: S.activation(rows(T.NT, k), T.NW[:, :].indirect(qd(T.TWL, k)), IDN), rnl, s_ce, v_tw[k]))
-        t_pt.append(wrap(3 + k, 64, T.D1, T.NT, 64 * k, s_nt[k], free[k]))
-
-    sdma("otn", T.TNH[:, :], lane(T.NN, 6), s_nn)
-    otn = sdma("otn", T.TNL[:, :], lane(T.NN, 7))
-    sdma("opt", T.PTH[:, :], lane(T.NT, 4), s_nt[3])
-    opt = sdma("opt", T.PTL[:, :], lane(T.NT, 5))
-
-    u, u2 = [], []
-    for k in range(4):
-        u.append(act(lambda: S.activation(rows(T.UX, k), T.MX[:, :].indirect(qd(T.TWL, k)), IDN), a1, v_m[3], v_tw[k]))
-        u2.append(sdma("u2%d" % k, rows(T.U2, k), rows(T.UX, k), u[k]))
-
-    v_t1 = vec(lambda: V.tensor_tensor(T.TMP[:, :], T.TNH[:, :], T.TNL[:, :], ADD), otn)
-    v_x1 = vec(lambda: V.tensor_scalar(T.NX[:, 1:1024:4], T.TMP[:, :], 4.0, 3.0, MUL, ADD), v_t1)
-    v_pt = [evac(qd(T.PTW, k), 3 + k, 64, t_pt[k]) for k in range(4)]
-    v_t2 = vec(lambda: V.tensor_tensor(T.TMP2[:, :], T.PTH[:, :], T.PTL[:, :], ADD), opt)
-    v_x2 = vec(lambda: V.tensor_scalar(T.NX[:, 2:1024:4], T.TMP2[:, :], 4.0, 2.0, MUL, ADD), v_t2)
-    sdma("stn", T.nx[:, :], T.NX[:, :], v_x0, v_x1, v_x2, v_x3)
-
-    for a, b in CHUNKS:
-        s_ye = act(lambda: S.activation(T.Y[:, 32 * a:32 * b:2], T.Q[:, :].indirect(T.NXW[:, a:b]), IDN), v_qa, v_qb)
-        v_yo = vec(lambda: V.tensor_tensor(T.Y[:, 32 * a + 1:32 * b:2], T.UX[:, :].indirect(T.PTW[:, a:b]), T.U2[:, 16 * a:16 * b],
-                                           ADD), a2, u2[a // 64], v_pt[a // 64], *u)
-        sdma("sty", T.y[:, 32 * a:32 * b], T.Y[:, 32 * a:32 * b], s_ye, v_yo)
+    def before(step):
+        name, a, b = step
+        names = STEP[name][0] + {"pt": pt_bank, "pn": pn_bank}.get(name, {a: (0,)})[a][1:]
+        return [s for s in every for n in names if s[0] == n.strip("*") and (n[-1] == "*" or (s[1] < b and a < s[2]))]
+    while any(queues.values()):
+        ready = [q for q in queues if queues[q] and all(s in done for s in before(queues[q][0]))]
+        step = queues[ready[0]].pop(0)
+        done[step] = STEP[step[0]][1](ready[0], step[1], step[2], [done[s] for s in before(step)])
 
     wait("g", g, [(s, total[s]) for s in total])

from concourse.bass import DstId, RemoteDMATransfer
from concourse.mybir import dt, AluOpType, ActivationFunctionType

H, E, NS = 4096, 64, 7
M = NS * E
HX = H + M
BFD, F32, I32, U16 = "bfloat16", "float32", "int32", "uint16"
SCRATCH = {"NX": ("sbuf", [128, 2, 128, 4], F32), "Y": ("sbuf", [128, 2 * H], BFD), "FA": ("sbuf", [128, 28], I32),
           "N0": ("sbuf", [128, 2, 2, 128], I32), "NF": ("sbuf", [128, 8, 32], F32), "NG": ("sbuf", [128, 256], F32),
           "NA": ("sbuf", [128, 3, 256], I32), "NH": ("sbuf", [128, 3, 256], BFD), "NL": ("sbuf", [128, 3, 256], BFD),
           "D": ("sbuf", [128, 4, 144], BFD), "BM": ("sbuf", [128, 4, 8], BFD), "LO": ("sbuf", [128, M], F32),
           "ID": ("sbuf", [128, 128], BFD), "NO": ("sbuf", [128, 4, 2, 128], BFD)}
for _k in ("X", "X2", "M1", "NN", "NT"):
    SCRATCH[_k] = ("sbuf", [128, H], BFD)
for _k in ("NW", "MX", "RX"):
    SCRATCH[_k] = ("sbuf", [128, HX], BFD)
for _k in ("LI", "LA"):
    SCRATCH[_k] = ("sbuf", [128, 4], I32)
for _k in ("LM", "HB", "KP"):
    SCRATCH[_k] = ("sbuf", [128, 4], F32)
for _k in ("C3", "R1", "RN", "XF", "MF", "EE", "VV"):
    SCRATCH[_k] = ("sbuf", [128, M], BFD)
for _k in ("FW", "NFW", "PFW", "EW"):
    SCRATCH[_k] = ("sbuf", [128, 32], U16)
for _k in ("NXW", "N2W", "TWL", "PTW"):
    SCRATCH[_k] = ("sbuf", [128, 256], U16)
for _k in range(8):
    SCRATCH["ps%d" % _k] = ("psum", [128, 512], F32)
SEMAPHORES = ["vec", "act", "ten", "gps", "ldb", "ldt", "ldp", "ld0", "ldf", "x0", "x1", "x2", "x3", "xc", "xm", "o0", "o1", "o2", "o3",
              "lan", "rnl", "stn", "sty", "a1", "an", "a2", "s1", "sn", "s2"]
ADD, SUB, MUL = AluOpType.add, AluOpType.subtract, AluOpType.mult
GE, IE = AluOpType.is_ge, AluOpType.is_equal
IDN = ActivationFunctionType.Identity
NEXT, PREV, CODE = 0, 1, 3
LOW = {1: 1, 4: 0}
PNUM, TWIN = 4, 8

VECTOR = ("m 0 128, m 128 256, mf, nn 200 256, pf_list, codes, n2_list 0 192, n2_list 192 256, nx0, ye 0 72, e_list, tw_list 0 64, "
          "nx3, vv, tw_list 64 160, r 0 56, tw_list 160 256, r 56 136, pt_list 0 64, r 136 200, r 200 256, pt_list 64 128, "
          "pt_list 128 192, ye 72 128, yo 104 144, pt_list 192 256, ye 128 192, ye 192 232, ye 232 256")
SCALAR = ("x2 0 64, x2 64 128, x2 128 192, r1, nn 0 64, nn 64 128, nn 128 200, m1 0 72, m1 72 152, ee, m1 152 256, nt 0 64, nt 64 128, "
          "nt 128 192, nt 192 256, nx1, nx2 0 128, yo 0 32, yo 32 72, yo 72 104, nx2 128 256, yo 144 192, yo 192 232, yo 232 256")
TENSOR = ("pf, n2 0 64, n2 64 128, n2 128 192, n2 192 256, tw 0 64, e, tw 64 160, tw 160 256, tn 0 128, tn 128 256, "
          "pt 0 64, pt 64 128, pt 128 192, pn 0 128, pt 192 256, pn 128 256")
GPSIMD = "send_numbers, send_m, send_r"
SYNC = ("x2 192 256, old_numbers, tn_out 0 128, tn_out 128 256, numbers_in, pn_out 0 128, pn_out 128 256, nx 0 128, y 0 32, y 32 72, "
        "y 72 128, nx 128 256, y 128 192, y 192 232, y 232 256")


def slot(r, q):
    return q - (1 if q > r else 0)


def steps(text):
    return [(w[0], int(w[1]), int(w[2])) if len(w) > 1 else (w[0], 0, 256) for w in (s.split() for s in text.split(","))]


def rank_program(g, core, T, topo):
    r = T.rank_of(core)
    if r is None:
        return
    base = H * r
    cores = T.cores
    total, seen = {}, {}

    def inc(op, s, n=1):
        op.then_inc(T.sem[s], n)
        total[s] = total.get(s, 0) + n
        return (s, total[s])

    def wait(qn, q, toks):
        best = {}
        for s, v in toks:
            best[s] = max(best.get(s, 0), v)
        for s in best:
            if seen.get((qn, s), 0) < best[s]:
                q.wait_ge(T.sem[s], best[s])
                seen[(qn, s)] = best[s]

    V, S, P, Y = g.vector, g.scalar, g.tensor, g.sync

    def vec(f, *toks):
        wait("v", V, toks)
        return inc(f(), "vec")

    def act(f, *toks):
        wait("s", S, toks)
        return inc(f(), "act")

    def gps(f, *toks):
        wait("g", g, toks)
        return inc(f(), "gps")

    def sdma(sem, out, in_, *toks):
        wait("y", Y, toks)
        return inc(Y.dma_start(out, in_), sem, 16)

    def ps(b, n, at=0):
        return T["ps%d" % b][:, at:at + n]

    def wrap(b, n, u, src, c0, *toks, at=0):
        wait("t", P, toks)
        for p in range(16):
            mm = P.matmul(ps(b, n, at), T.D[:, u, 15 - p:143 - p], src[:, 16 * c0 + p:16 * (c0 + n):16], p == 0, p == 15)
        return inc(mm, "ten")

    def pair_out(j, src, k, a, b, *toks):
        for d in range(2):
            tok = sdma("o%d" % j, T.NO[:, j, d], src[k + d:128:16, 16 * a:16 * b], *toks)
        return tok

    def pair_sum(b, at, j, *toks):
        wait("t", P, toks)
        for d in range(2):
            mm = P.matmul(ps(b, 128, at), T.ID[:, :], T.NO[:, j, d], d == 0, d == 1)
        return inc(mm, "ten")

    def evac(out, src, *toks):
        return vec(lambda: V.tensor_scalar(out, src, float(base), None, SUB), *toks)

    def lane(t, k):
        return t[k:128:16, 0:H]

    def rows(t, k):
        return t[:, 1024 * k:1024 * k + 1024]

    def cols(t, a, b):
        return t[:, 16 * a:16 * b]

    def take(q, out, win, lst, *toks):
        if q == "v":
            return vec(lambda: V.tensor_copy(out, win.indirect(lst)), *toks)
        return act(lambda: S.activation(out, win.indirect(lst), IDN), *toks)

    def vsum(out, win, lst, in1, *toks):
        return vec(lambda: V.tensor_tensor(out, win.indirect(lst), in1, ADD), *toks)

    far = T.FW[:, 0:28]
    X, MX, ML, NW, NWL = T.X[:, :], T.MX[:, :], T.MX[:, 0:H], T.NW[:, :], T.NW[:, 0:H]

    ldt = sdma("ldt", T.NA[:, 2], T.twn[:, :])
    inc(S.dma_start(T.NA[:, 0, 0:128], T.nxt[0:8:2, :]), "ldb", 16)
    ldb = sdma("ldb", T.NA[:, 0, 128:256], T.nxt[1:8:2, :])
    ldp = inc(S.dma_start(T.NA[:, 1], T.prv[:, :]), "ldp", 16)
    ldf = inc(S.dma_start(T.FA[:, :], T.far[:, :]), "ldf", 16)
    xs = [sdma("x%d" % k, rows(T.X, k), rows(T.x, k)) for k in range(4)]

    def iot(ap, pat, b, *toks):
        return gps(lambda: g.iota(ap, pat, b, 0, allow_small_or_imprecise_dtypes=True), *toks)

    g_li = gps(lambda: g.iota(T.LI[:, :], [[-8, 2], [-1, 2]], 14, 1))
    g_lo = iot(T.LO[:, :], [[1, M]], -256)
    g_one = iot(T.BM[:, :, :], [[0, 32]], 1)
    g_b = gps(lambda: g.affine_select(T.BM[:, :, :], T.BM[:, :, :], [[-8, 2], [-2, 2], [-16, 8]], GE, 0.0, 0, 1), g_one)
    g_hi = {k: gps(lambda: g.affine_select(T.NH[:, k], T.NA[:, k], [[0, 256]], GE, 0.0, 0, 0), ld) for k, ld in ((2, ldt), (1, ldp), (0, ldb))}

    v_nw = vec(lambda: V.memset(T.NW[:, 0:1024], 0.0))
    vec(lambda: V.memset(T.NW[:, 1024:3072], 0.0))
    v_la = vec(lambda: V.tensor_scalar(T.LA[:, :], T.LI[:, :], 15, None, AluOpType.bitwise_and), g_li)
    vec(lambda: V.tensor_scalar(T.LM[:, :], T.LA[:, :], 0.0, None, IE), v_la)
    vec(lambda: V.tensor_scalar(T.KP[:, 0:1], T.LA[:, 2:3], 2.0, None, GE))
    v_hb = vec(lambda: V.tensor_scalar(T.HB[:, :], T.LA[:, :], 0.0, float(base + H + 256), IE, MUL))

    act(lambda: S.activation(T.NW[:, 3072:H], T.NW[:, 0:1024], IDN), v_nw)
    s_d0 = act(lambda: S.activation(T.D[:, :, :], T.NW[:, 0:576], IDN))
    s_c3 = act(lambda: S.activation(T.C3[:, :], T.LO[:, :], IDN, bias=T.HB[:, 2:3], scale=T.LM[:, 3:4]), v_hb, g_lo)
    s_ce = act(lambda: S.activation(T.NW[:, H:HX], T.LO[:, :], IDN, bias=T.HB[:, 0:1], scale=T.LM[:, 1:2]))
    g_d = gps(lambda: g.affine_select(T.D[:, :, 15:128:16], T.BM[:, :, :], [[8, 2], [2, 2], [16, 8]], GE, 0.0, 1, -1), g_b, s_d0)
    g_i1 = iot(T.ID[:, :], [[0, 128]], 1)
    g_id = gps(lambda: g.affine_select(T.ID[:, :], T.ID[:, :], [[-1, 128]], IE, 0.0, 0, 1), g_i1)

    def low(k):
        return vec(lambda: V.tensor_tensor(T.NL[:, k], T.NA[:, k], T.NH[:, k], SUB), g_hi[k])
    for e in range(2):
        v_f = vec(lambda: V.tensor_scalar(T.NF[:, :, 16 * e:16 * e + 16], T.NA[:, 0, 128 * e:128 * e + 128], float(base), None, SUB), ldb)
    v_lo = {2: low(2)}
    v_fw = vec(lambda: V.tensor_copy(far, T.FA[:, :]), ldf)
    for b in range(8):
        v_g = vec(lambda: V.transpose(T.NG[:, b:256:8], T.NF[:, b, :]), v_f)
        if b in LOW:
            v_lo[LOW[b]] = low(LOW[b])
    v_nq = vec(lambda: V.tensor_copy(T.NXW[:, :], T.NG[:, :]), v_g)
    for j, ks in ((2, (TWIN, 10)), (1, (2, PNUM)), (0, ())):
        for d, t, tok in ((0, T.NH, g_hi[j]), (1, T.NL, v_lo[j])):
            if j == 0:
                for e in range(2):
                    lan = sdma("lan", T.NW[16 * e + d:128:32, 0:H], t[:, 0, 128 * e:128 * e + 128], tok)
            for k in ks:
                sdma("lan", lane(T.NW, k + d), t[:, j], tok, s_d0, v_hb)

    def second_x(q, a, b):
        if q == "y":
            return sdma("xc", cols(T.X2, a, b), cols(T.x, a, b))
        return act(lambda: S.activation(cols(T.X2, a, b), cols(T.X, a, b), IDN), *xs[a // 64:(b - 1) // 64 + 1])

    def add_x(a, b, *toks):
        wait("g", g, toks)
        return inc(g.dma_start(cols(T.MX, a, b), cols(T.x, a, b), accum_op=ADD), "xm", 16)

    def old_numbers():
        for j, t in enumerate((T.nxt, T.prv)):
            for h in range(2):
                tok = sdma("ld0", T.N0[:, j, h], t[:, 2048 * h:2048 * h + 2048])
        return tok

    def order():
        used, plan = [], []
        away = [q for q in range(8) if q != r and topo.chip(cores[q]) != topo.chip(core)]
        near = [q for q in range(8) if q != r and topo.chip(cores[q]) == topo.chip(core)]
        for q in away + near:
            es = topo.engines(core, cores[q])
            es = es[::2] + es[1::2]
            e = [k for k in es if k not in used][0]
            used.append(e)
            plan.append((q, e))
        return plan
    plan = order()

    def send(src, dst, d0, rs, ls, *toks):
        wait("g", g, toks)
        tr = []
        for q, e in plan:
            rid, pid, _se = topo.addr(cores[q])
            i, k = slot(r, q), slot(q, r)
            tr.append(RemoteDMATransfer(dst_ids=[DstId(rid=rid, pnc=pid)], dma_engine_mask=1 << e, remote_sem=T.sem[rs],
                                        src=src[:, E * i:E * i + E], dst=dst[:, d0 + E * k:d0 + E * k + E]))
        g.remote_dma_fused(tr, local_sem=T.sem[ls])
        total[ls] = NS
        total[rs] = NS
        return (ls, NS)
    a1, an, a2 = ("a1", NS), ("an", NS), ("a2", NS)

    def numbers_in():
        sdma("rnl", T.NW[PNUM:128:16, H:HX], T.RN[2:128:16, :], an, s_ce)
        return sdma("rnl", T.NW[PNUM + 1:128:16, H:HX], T.RN[3:128:16, :])

    queues = {"v": steps(VECTOR), "s": steps(SCALAR), "t": steps(TENSOR), "g": steps(GPSIMD), "y": steps(SYNC)}
    every = [s for q in queues for s in queues[q]]
    tw_bank = dict(zip([s[1] for s in queues["t"] if s[0] == "tw"], (2, 3, 7)))
    pt_bank = {0: (1, "pf_list*"), 64: (2, "tw_list*"), 128: (3, "tw_list*"), 192: (4, "n2_list*")}
    pn_bank = {0: (5, "n2_list*"), 128: (7, "tw_list*")}

    def n2_bank(a):
        return (4, a) if a < 192 else (5, 0)
    nxt_list, tw_list = (lambda a, b: T.NXW[:, a:b]), (lambda a, b: T.TWL[:, a:b])
    STEP = {
        "x2": ((), lambda q, a, b, t: second_x(q, a, b)),
        "x1": ((), lambda q, a, b, t: take(q, cols(T.MX, a, b), X, nxt_list(a, b), v_nq, *xs)),
        "m": (("x2", "x1"), lambda q, a, b, t: vsum(cols(T.MX, a, b), X, nxt_list(a, b), cols(T.X2, a, b), v_nq, *xs, *t) if q == "v"
              else add_x(a, b, *t)),
        "old_numbers": ((), lambda q, a, b, t: old_numbers()),
        "r1": ((), lambda q, a, b, t: act(lambda: S.activation(T.R1[:, :], NWL.indirect(far), IDN, scale=T.KP[:, 0:1]), lan, v_fw)),
        "nn": ((), lambda q, a, b, t: take(q, cols(T.NN, a, b), NWL, nxt_list(a, b), lan, v_nq)),
        "mf": (("m",), lambda q, a, b, t: take(q, T.MF[:, :], ML, far, *t)),
        "xf": ((), lambda q, a, b, t: take(q, T.XF[:, :], X, far, v_fw, *xs)),
        "mf_early": (("xf", "nf_list"), lambda q, a, b, t: vsum(T.MF[:, :], X, T.NFW[:, 0:28], T.XF[:, :], *t)),
        "codes": (("r1", "nn"), lambda q, a, b, t: vec(lambda: V.tensor_tensor(NWL.indirect(far), T.R1[:, :], T.C3[:, :], ADD), s_c3, *t)),
        "m1": (("m*",), lambda q, a, b, t: take(q, cols(T.M1, a, b), ML, nxt_list(a, b), *t)),
        "ee": (("pf_list", "codes"), lambda q, a, b, t: take(q, T.EE[:, :], NWL, T.PFW[:, 0:28], *t)),
        "vv": (("e_list", "mf", "mf_early", "m"), lambda q, a, b, t: vsum(T.VV[:, :], MX, T.EW[:, 0:28], T.MF[:, :], a1, *t)),
        "ye": (("m1", "n2_list"), lambda q, a, b, t: vsum(T.Y[:, 32 * a:32 * b:2], ML, T.N2W[:, a:b], cols(T.M1, a, b), *t)),
        "r": (("m1", "tw_list"), lambda q, a, b, t: vsum(cols(T.RX, a, b), MX, tw_list(a, b), cols(T.M1, a, b), a1, *t)),
        "nt": (("tw_list", "numbers_in"), lambda q, a, b, t: take(q, cols(T.NT, a, b), NW, tw_list(a, b), *t)),
        "yo": (("r*", "pt_list"), lambda q, a, b, t: take(q, T.Y[:, 32 * a + 1:32 * b:2], T.RX[:, :], T.PTW[:, a:b], a2, *t)),
        "nx0": (("old_numbers",), lambda q, a, b, t: vec(lambda: V.tensor_scalar(T.NX[:, :, :, 0], T.N0[:, 0], 4.0, None, MUL), *t)),
        "nx3": (("old_numbers",), lambda q, a, b, t: vec(lambda: V.tensor_scalar(T.NX[:, :, :, 3], T.N0[:, 1], 4.0, 1.0, MUL, ADD), *t)),
        "nx1": (("tn",), lambda q, a, b, t: act(lambda: S.activation(T.NX[:, :, :, 1], ps(0, 256), IDN, bias=3.0, scale=4.0), *t)),
        "nx2": (("pn",), lambda q, a, b, t: act(lambda: S.activation(T.NX[:, a // 128, :, 2], ps(pn_bank[a][0], 128), IDN,
                                                                     bias=2.0, scale=4.0), *t)),
        "nf": (("r1",), lambda q, a, b, t: wrap(6, 28, NEXT, T.R1, 0, g_d, *t)),
        "pf": (("r1",), lambda q, a, b, t: wrap(1, 28, PREV, T.R1, 0, g_d, *t)),
        "e": (("ee", "nf_list"), lambda q, a, b, t: wrap(6, 28, CODE, T.EE, 0, *t)),
        "n2": (("nn",), lambda q, a, b, t: wrap(n2_bank(a)[0], b - a, NEXT, T.NN, a, *t, at=n2_bank(a)[1])),
        "tw": (("codes",), lambda q, a, b, t: wrap(tw_bank[a], b - a, CODE, T.NW, a, *t)),
        "pt": (("nt",), lambda q, a, b, t: wrap(pt_bank[a][0], b - a, PREV, T.NT, a, *t)),
        "tn": (("tn_out",), lambda q, a, b, t: pair_sum(0, a, a // 128, g_id, *t)),
        "pn": (("pn_out",), lambda q, a, b, t: pair_sum(pn_bank[a][0], 0, 2 + a // 128, *t)),
        "nf_list": (("nf",), lambda q, a, b, t: evac(T.NFW[:, 0:28], ps(6, 28), *t)),
        "pf_list": (("pf",), lambda q, a, b, t: evac(T.PFW[:, 0:28], ps(1, 28), *t)),
        "e_list": (("e",), lambda q, a, b, t: evac(T.EW[:, 0:28], ps(6, 28), *t)),
        "n2_list": (("n2",), lambda q, a, b, t: evac(T.N2W[:, a:b], ps(n2_bank(a)[0], b - a), *t)),
        "tw_list": (("tw",), lambda q, a, b, t: evac(T.TWL[:, a:b], ps(tw_bank[a], b - a), *t)),
        "pt_list": (("pt",), lambda q, a, b, t: evac(T.PTW[:, a:b], ps(pt_bank[a][0], b - a), *t)),
        "send_numbers": (("r1",), lambda q, a, b, t: send(T.R1, T.RN, 0, "an", "sn", *t)),
        "send_m": (("mf", "mf_early"), lambda q, a, b, t: send(T.MF, T.MX, H, "a1", "s1", *t)),
        "send_r": (("vv",), lambda q, a, b, t: send(T.VV, T.RX, H, "a2", "s2", *t)),
        "numbers_in": ((), lambda q, a, b, t: numbers_in()),
        "tn_out": (("nn",), lambda q, a, b, t: pair_out(a // 128, T.NN, TWIN, a, b, *t)),
        "pn_out": (("nt",), lambda q, a, b, t: pair_out(2 + a // 128, T.NT, PNUM, a, b, *t)),
        "y": (("ye", "yo"), lambda q, a, b, t: sdma("sty", T.y[:, 32 * a:32 * b], T.Y[:, 32 * a:32 * b], *t)),
        "nx": (("nx0", "nx1", "nx2", "nx3"), lambda q, a, b, t: sdma("stn", T.nx[:, 64 * a:64 * b], T.NX[:, a // 128], *t)),
    }
    done = {}

    def before(step):
        name, a, b = step
        names = STEP[name][0] + {"pt": pt_bank, "pn": pn_bank}.get(name, {a: (0,)})[a][1:]
        return [s for s in every for n in names if s[0] == n.strip("*") and (n[-1] == "*" or (s[1] < b and a < s[2]))]
    while any(queues.values()):
        ready = [q for q in queues if queues[q] and all(s in done for s in before(queues[q][0]))]
        step = queues[ready[0]].pop(0)
        done[step] = STEP[step[0]][1](ready[0], step[1], step[2], [done[s] for s in before(step)])

    wait("g", g, [(s, total[s]) for s in total])
